import numpy as np
import ml_dtypes


def mxq(x, axis, fmt="e4m3"):
    dtype, down = {"e4m3": (ml_dtypes.float8_e4m3fn, 7), "e5m2": (ml_dtypes.float8_e5m2, 14)}[fmt]
    v = np.moveaxis(np.asarray(x, np.float32).astype(ml_dtypes.bfloat16).astype(np.float64), axis, -1)
    blocks = v.reshape(v.shape[:-1] + (-1, 32))
    amax = np.abs(blocks).max(-1, keepdims=True)
    byte = np.maximum(np.where(amax > 0, np.frexp(amax)[1] - 1 + 127, 0) - down, 1)
    scale = np.exp2(byte - 127.0)
    codes = (blocks / scale).astype(np.float32).astype(dtype).astype(np.float64)
    return np.moveaxis((codes * scale).reshape(v.shape), -1, axis)


WIDE = False


def mx_kscale(k):
    if not WIDE:
        return np.ones(k)
    levels = np.array([10, -10, 5, -5, 0])
    if k % 512:
        return np.exp2(np.random.permutation(np.resize(levels, k // 32))).repeat(32)
    a = np.empty((k // 512, 16))
    for p in range(k // 512):
        a[p, :8] = np.random.permutation(np.resize(levels, 8))
        for g in range(8):
            far = levels[np.abs(levels - a[p, g]) >= 10]
            a[p, g + 8] = far[np.random.randint(len(far))]
    return np.exp2(a.ravel()).repeat(32)


def f64(x):
    return np.asarray(x).astype(np.float64)


def striped(idx):
    return np.tile(np.asarray(idx).reshape(-1, 16).T, (8, 1)).astype(np.uint16)


def unstriped(offs):
    return offs[:16].T.reshape(-1).astype(np.int64)


def striped8(idx):
    return np.asarray(idx).reshape(8, -1, 16).transpose(0, 2, 1).reshape(128, -1).astype(np.uint16)


def unstriped8(offs):
    return offs.reshape(8, 16, -1).transpose(0, 2, 1).reshape(8, -1).astype(np.int64)


def pick8(x, idx, run):
    r = np.arange(len(x))
    return x[r[:, None], idx[r % (8 * run) // run]]


E2M1 = np.array([0.0, 0.5, 1.0, 1.5, 2.0, 3.0, 4.0, 6.0, -0.0, -0.5, -1.0, -1.5, -2.0, -3.0, -4.0, -6.0])


def pack_weight(w, fmt):
    k, n = w.shape
    w = f64(np.asarray(w, np.float32).astype(ml_dtypes.bfloat16)).reshape(k // 32, 32, n)
    amax = np.abs(w).max(1)
    if fmt == "e4m3":
        byte = np.frexp(amax)[1] - 1 + 127 - 7
    else:
        mant, ex = np.frexp(amax / 6.0)
        byte = np.where(mant > 0.5, ex, ex - 1) + 127
    byte = np.clip(np.where(amax > 0, byte, 1), 1, 254)
    scaled = (w * np.exp2(127.0 - byte)[:, None, :]).reshape(k, n).astype(np.float32)
    by_word = np.ascontiguousarray(scaled.reshape(k // 512, 128, 4, n).transpose(0, 1, 3, 2))
    if fmt == "e4m3":
        words = by_word.astype(ml_dtypes.float8_e4m3fn).view(np.uint8)
    else:
        c = by_word.astype(ml_dtypes.float4_e2m1fn).view(np.uint8) & 0xF
        words = (c[..., 0::2] | (c[..., 1::2] << 4)).reshape(k // 512, 128, 2 * n)
    return np.ascontiguousarray(words), np.ascontiguousarray(byte.astype(np.uint8).reshape(k // 512, 16, n))


def unpack_weight(words, scales, fmt):
    g, _, n = scales.shape
    words = np.ascontiguousarray(words).reshape(g, 128, n, -1)
    if fmt == "e4m3":
        vals = words.view(ml_dtypes.float8_e4m3fn).astype(np.float64)
    else:
        nib = np.empty((g, 128, n, 4), np.uint8)
        nib[..., 0::2] = words & 0xF
        nib[..., 1::2] = words >> 4
        vals = E2M1[nib]
    vals = vals * np.repeat(np.exp2(scales.astype(np.float64) - 127.0), 8, axis=1)[..., None]
    return vals.transpose(0, 1, 3, 2).reshape(g * 512, n)


K, J, R, T, U, Z, M, O, N = 512, 256, 512, 512, 512, 512, 1024, 128, 256


def setup_inputs():
    n = np.random.standard_normal
    idx = np.stack([np.random.permutation(T)[:J] for _ in range(8)])
    idx2 = np.stack([np.random.permutation(U)[:J] for _ in range(8)])
    idx3 = np.stack([np.random.permutation(U)[:J] for _ in range(8)])
    idx4 = np.random.permutation(M)[:J]
    idx5 = np.stack([np.random.permutation(J)[:O] for _ in range(8)])
    idx6 = np.random.permutation(J)[:O]
    idx7 = np.stack([np.random.permutation(J)[:O] for _ in range(8)])
    fk = mx_kscale(K)
    fr = mx_kscale(R)
    fz = mx_kscale(Z)
    wp = pack_weight(n((K, R)) * 1 / np.sqrt(K) / fk[:, None] * fr, "e2m1")
    xop = pack_weight(n((Z, M)) / fz[:, None], "e2m1")
    w2p = pack_weight(n((Z, R)) * 1 / np.sqrt(Z) * fz[:, None] * fr, "e4m3")
    wbp = pack_weight(n((R, N)) * 1 / np.sqrt(R) / fr[:, None], "e4m3")
    return {
        "ta": (np.random.randint(-7, 8, (K, T)).astype(np.float64)).astype(np.float32),
        "ga": ((np.random.randint(8, 25, (K, 1)) / 64.0) * fk[:, None]).astype(np.float32),
        "gb": (np.random.uniform(0.5, 1.6, (K, 1))).astype(np.float32),
        "w_words": wp[0],
        "w_scales": wp[1],
        "xo_words": xop[0],
        "xo_scales": xop[1],
        "w2_words": w2p[0],
        "w2_scales": w2p[1],
        "sa": (np.random.uniform(0.5, 1.6, (R, 1))).astype(np.float32),
        "sb": (np.random.uniform(0.5, 1.6, (R, 1))).astype(np.float32),
        "sd": (np.random.uniform(0.5, 1.6, (R, 1))).astype(np.float32),
        "wb_words": wbp[0],
        "wb_scales": wbp[1],
        "offs": striped8(idx),
        "offs2": striped8(idx2),
        "offs3": striped8(idx3),
        "offs4": striped(idx4),
        "offs5": striped8(idx5),
        "offs6": striped(idx6),
        "offs7": striped8(idx7),
    }


def reference(ta, ga, gb, w_words, w_scales, xo_words, xo_scales, w2_words, w2_scales, sa, sb, sd, wb_words, wb_scales, offs, offs2, offs3, offs4, offs5, offs6, offs7):
    idx = unstriped8(offs)
    idx2 = unstriped8(offs2)
    idx3 = unstriped8(offs3)
    idx4 = unstriped(offs4)
    idx5 = unstriped8(offs5)
    idx6 = unstriped(offs6)
    idx7 = unstriped8(offs7)
    wu = unpack_weight(w_words, w_scales, "e2m1")
    xou = unpack_weight(xo_words, xo_scales, "e2m1")
    w2u = unpack_weight(w2_words, w2_scales, "e4m3")
    wbu = unpack_weight(wb_words, wb_scales, "e4m3")
    xcd = pick8(f64(ta), idx, 64) * f64(ga)
    xcp = np.zeros((K, U))
    xcp[np.arange(K)[:, None], idx2[np.arange(K) % 512 // 64]] = xcd
    xc = pick8(xcp, idx3, 64) * f64(gb)
    xcq = mxq(xc, 0, "e4m3")
    a = wu.T @ xcq
    xoidx4g = xou[:, idx4]
    b = w2u.T @ xoidx4g
    hid = np.maximum(pick8(a, idx5, 64) * f64(sa), a[:, idx6] * f64(sb)) - pick8(b, idx7, 64) * f64(sd)
    hidq = mxq(hid, 0, "e4m3")
    y = wbu.T @ hidq
    return y

@@ -1,0 +1,228 @@
+from contextlib import ExitStack
+
+import concourse.mybir as mybir
+
+K, J, R, T, U, Z, M, O, N = 512, 256, 512, 512, 512, 512, 1024, 128, 256
+FLOPS = 2 * (K * R * J + Z * R * J + R * N * O)
+
+F32 = mybir.dt.float32
+BF16 = mybir.dt.bfloat16
+I32 = mybir.dt.int32
+U32 = mybir.dt.uint32
+U16 = mybir.dt.uint16
+U8 = mybir.dt.uint8
+FP8X4 = mybir.dt.float8_e4m3fn_x4
+FP4X4 = mybir.dt.float4_e2m1fn_x4
+COPY = mybir.ActivationFunctionType.Copy
+ALU = mybir.AluOpType
+
+P = 128
+PACK = 4
+QUADRANTS = 4
+HALF = J // 2
+RUN = 4
+
+
+def tile_picked_codepage_plain_two_crossgroups_one_plain_kernel(
+    tc, ta, ga, gb, w_words, w_scales, xo_words, xo_scales, w2_words, w2_scales, sa, sb, sd,
+    wb_words, wb_scales, offs, offs2, offs3, offs4, offs5, offs6, offs7, out,
+):
+    nc = tc.nc
+    with ExitStack() as ctx:
+        lists = ctx.enter_context(tc.tile_pool(name="lists", bufs=1))
+        keep = ctx.enter_context(tc.tile_pool(name="keep", bufs=1))
+        late = ctx.enter_context(tc.tile_pool(name="late", bufs=1))
+        psum = ctx.enter_context(tc.psum_pool(name="psum", bufs=1))
+
+        def load_list(name, source):
+            held = lists.tile(list(source.shape), U16, name=name)
+            nc.sync.dma_start(held[:], source)
+            return held
+
+        def load_factor(name, source):
+            held = keep.tile([P, PACK], F32, name=name)
+            nc.sync.dma_start(out=held[:], in_=source.rearrange("(p t) one -> p (t one)", t=PACK))
+            return held
+
+        def load_table(t):
+            held = late.tile([P, T], F32, name="table%d" % t, offset=4 * T * (PACK - 1 - t))
+            nc.sync.dma_start(out=held[:], in_=ta.rearrange("(p t) c -> p t c", t=PACK)[:, t, :])
+            return held
+
+        def load_words(name, source, columns, dtype):
+            held = keep.tile([P, columns], dtype, name=name, tag=name, align_bytes=64)
+            nc.sync.dma_start(out=held[:].bitcast(I32), in_=source.bitcast(I32))
+            return held
+
+        def zeroed_scales(engine, name, columns):
+            held = keep.tile([P, columns], U8, name=name, tag=name, align_bytes=64)
+            engine.memset(held[:].bitcast(I32), 0)
+            return held
+
+        def load_scales(held, source, quadrants):
+            for q in quadrants:
+                nc.sync.dma_start(
+                    out=held[32 * q : 32 * q + 4, :].bitcast(I32),
+                    in_=source[0, 4 * q : 4 * q + 4, :].bitcast(I32),
+                )
+
+        def fetch(target, window, offsets, factor, t):
+            nc.scalar.activation(
+                out=target, in_=window[:].indirect(offsets), func=COPY, scale=factor[:, t : t + 1]
+            )
+
+        def dealt(copy, name, tag, source, dtype):
+            held = keep.tile([P, R], dtype, name=name, tag=tag, align_bytes=64)
+            copy(
+                out=held[:].rearrange("p (t m) -> p m t", t=PACK),
+                in_=source[:].rearrange("p (m t) -> p m t", t=PACK),
+            )
+            return held
+
+        xo_scale_rows = zeroed_scales(nc.gpsimd, "xo_scale_rows", M)
+        w2_scale_rows = zeroed_scales(nc.vector, "w2_scale_rows", R)
+        w_scale_rows = zeroed_scales(nc.gpsimd, "w_scale_rows", R)
+        wb_scale_rows = zeroed_scales(nc.vector, "wb_scale_rows", N)
+        pages = [keep.tile([P, U], F32, name="page%d" % t) for t in range(PACK)]
+        for page in pages:
+            nc.vector.memset(page[:], 0.0)
+
+        tables = [load_table(0)]
+        code_list = load_list("code_list", offs)
+        step = load_factor("step", ga)
+        put_list = load_list("put_list", offs2)
+        tables.append(load_table(1))
+        reading = load_factor("reading", gb)
+        read_list = load_list("read_list", offs3)
+        w2_raw = load_words("w2_raw", w2_words[0].rearrange("p c t -> p (c t)"), R, U32)
+        w_raw = load_words("w_raw", w_words[0], R, U16)
+        load_scales(xo_scale_rows, xo_scales, range(QUADRANTS))
+        load_scales(w2_scale_rows, w2_scales, (0, 1))
+        xo_all = load_words("xo_all", xo_words[0], M, U16)
+        load_scales(w2_scale_rows, w2_scales, (2, 3))
+        note_list = load_list("note_list", offs4)
+        tables.append(load_table(2))
+        tables.append(load_table(3))
+        load_scales(w_scale_rows, w_scales, range(QUADRANTS))
+        off_list = load_list("off_list", offs7)
+        third_weight = load_factor("third_weight", sd)
+        own_list = load_list("own_list", offs5)
+        first_weight = load_factor("first_weight", sa)
+        shared_list = load_list("shared_list", offs6)
+        second_weight = load_factor("second_weight", sb)
+        wb_codes = load_words("wb_codes", wb_words[0].rearrange("p c t -> p (c t)"), N, U32)
+        load_scales(wb_scale_rows, wb_scales, range(QUADRANTS))
+
+        def fetch_codes(xcd, t):
+            fetch(xcd[:, t % 2, :], tables[t], code_list[:], step, t)
+
+        def put_codes(xcd, t):
+            nc.vector.tensor_copy(out=pages[t][:].indirect(put_list[:]), in_=xcd[:, t % 2, :])
+
+        def read_page(t):
+            for h in range(2):
+                fetch(xc_planes[h][:, t, :], pages[t], read_list[:, 8 * h : 8 * h + 8], reading, t)
+
+        xcd_early = keep.tile([P, 2, J], F32, name="xcd_early")
+        for t in (0, 1):
+            fetch_codes(xcd_early, t)
+            put_codes(xcd_early, t)
+        w2_codes = dealt(nc.scalar.copy, "w2_codes", "w2_codes", w2_raw, U32)
+        w_codes = dealt(nc.scalar.copy, "w_codes", "w_codes", w_raw, U16)
+        xc_flat = keep.tile([P, PACK * J], BF16, name="xc_flat", tag="w_raw", align_bytes=64)
+        xc_planes = [
+            xc_flat[:, PACK * HALF * h : PACK * HALF * (h + 1)].rearrange("p (t c) -> p t c", t=PACK) for h in range(2)
+        ]
+        for t in (0, 1):
+            read_page(t)
+
+        w2_plane = dealt(nc.vector.tensor_copy, "w2_plane", "w2_plane", w2_scale_rows, U8)
+        note_scales = keep.tile([P, J], U8, name="note_scales", align_bytes=64)
+        nc.vector.tensor_copy(out=note_scales[:], in_=xo_scale_rows[:].indirect(note_list[:]))
+        note_codes = keep.tile([P, J], U16, name="note_codes", align_bytes=64)
+        nc.vector.tensor_copy(out=note_codes[:], in_=xo_all[:].indirect(note_list[:]))
+        xcd_late = keep.tile([P, 2, J], F32, name="xcd_late", tag="w2_scale_rows", align_bytes=64)
+        for t in (2, 3):
+            fetch_codes(xcd_late, t)
+            put_codes(xcd_late, t)
+
+        b_rows = []
+        for t in range(PACK):
+            cols = slice(P * t, P * (t + 1))
+            bank = psum.tile([P, J], F32, name="b_bank%d" % t, tag="bank%d" % t)
+            nc.tensor.matmul_mx(
+                out=bank[:],
+                lhsT=w2_codes[:, cols].bitcast(FP8X4), lhsT_scale=w2_plane[:, cols],
+                rhs=note_codes[:].bitcast(FP4X4), rhs_scale=note_scales[:],
+                start=True, stop=True,
+            )
+            rows = late.tile([P, J], F32, name="b_rows%d" % t, offset=4 * J * t)
+            nc.scalar.copy(out=rows[:], in_=bank[:])
+            b_rows.append(rows)
+
+        for t in (2, 3):
+            read_page(t)
+        w_plane = dealt(nc.vector.tensor_copy, "w_plane", "w2_scale_rows", w_scale_rows, U8)
+        grouped = [keep.tile([P, HALF, PACK], BF16, name="xc_grouped%d" % h, align_bytes=64) for h in range(2)]
+        xc_codes = keep.tile([P, J], U32, name="xc_codes", align_bytes=64)
+        xc_scales = keep.tile([P, J], U8, name="xc_scales", align_bytes=64)
+        for h in range(2):
+            nc.vector.tensor_copy(
+                out=grouped[h][:].rearrange("p (c i) t -> p c t i", i=RUN),
+                in_=xc_planes[h].rearrange("p t (c i) -> p c t i", i=RUN),
+            )
+        for h in range(2):
+            nc.vector.quantize_mx(
+                out=xc_codes[:, HALF * h : HALF * (h + 1)].bitcast(FP8X4),
+                scales=xc_scales[:, HALF * h : HALF * (h + 1)],
+                in_=grouped[h][:].rearrange("p c t -> p (c t)"),
+            )
+
+        taken_off = keep.tile([P, PACK, O], F32, name="taken_off")
+        for t in range(PACK):
+            fetch(taken_off[:, t, :], b_rows[t], off_list[:], third_weight, t)
+
+        own = keep.tile([P, PACK, O], F32, name="own")
+        shared = keep.tile([P, PACK, O], F32, name="shared")
+        larger = keep.tile([P, PACK, O], F32, name="larger")
+        for t in range(PACK):
+            cols = slice(P * t, P * (t + 1))
+            bank = psum.tile([P, J], F32, name="a_bank%d" % t, tag="bank%d" % (PACK + t))
+            nc.tensor.matmul_mx(
+                out=bank[:],
+                lhsT=w_codes[:, cols].bitcast(FP4X4), lhsT_scale=w_plane[:, cols],
+                rhs=xc_codes[:].bitcast(FP8X4), rhs_scale=xc_scales[:],
+                start=True, stop=True,
+            )
+            rows = keep.tile([P, J], F32, name="a_rows%d" % t)
+            nc.vector.tensor_copy(out=rows[:], in_=bank[:])
+            fetch(own[:, t, :], rows, own_list[:], first_weight, t)
+            fetch(shared[:, t, :], rows, shared_list[:], second_weight, t)
+        hid = keep.tile([P, O, PACK], BF16, name="hid", align_bytes=64)
+        for pair in (slice(0, 2), slice(2, 4)):
+            for t in range(pair.start, pair.stop):
+                nc.vector.tensor_tensor(out=larger[:, t, :], in0=own[:, t, :], in1=shared[:, t, :], op=ALU.max)
+            nc.vector.tensor_tensor(
+                out=hid[:, :, pair].rearrange("p (c i) t -> p c t i", i=RUN),
+                in0=larger[:, pair, :].rearrange("p t (c i) -> p c t i", i=RUN),
+                in1=taken_off[:, pair, :].rearrange("p t (c i) -> p c t i", i=RUN),
+                op=ALU.subtract,
+            )
+        hid_codes = keep.tile([P, O], U32, name="hid_codes", align_bytes=64)
+        hid_scales = keep.tile([P, O], U8, name="hid_scales", align_bytes=64)
+        nc.vector.quantize_mx(
+            out=hid_codes[:].bitcast(FP8X4), scales=hid_scales[:], in_=hid[:].rearrange("p c t -> p (c t)")
+        )
+
+        for h, (copy, queue) in enumerate(((nc.vector.tensor_copy, nc.sync), (nc.scalar.copy, nc.scalar))):
+            cols = slice(P * h, P * (h + 1))
+            bank = psum.tile([P, O], F32, name="y_bank%d" % h, tag="bank%d" % h)
+            nc.tensor.matmul_mx(
+                out=bank[:],
+                lhsT=wb_codes[:, cols].bitcast(FP8X4), lhsT_scale=wb_scale_rows[:, cols],
+                rhs=hid_codes[:].bitcast(FP8X4), rhs_scale=hid_scales[:],
+                start=True, stop=True,
+            )
+            result = keep.tile([P, O], F32, name="result%d" % h)
+            copy(out=result[:], in_=bank[:])
+            queue.dma_start(out=out[cols, :], in_=result[:])

@@ -79,6 +79,9 @@ def tile_picked_codepage_plain_two_crossgroups_one_plain_kernel(
             )
             return held
 
+        idle = keep.tile([P, 16], F32, name="idle")
+        nc.gpsimd.memset(idle[:], 0.0)
+        nc.scalar.activation(out=idle[:, 8:9], in_=idle[:, 0:1], func=COPY)
         xo_scale_rows = zeroed_scales(nc.gpsimd, "xo_scale_rows", M)
         w2_scale_rows = zeroed_scales(nc.vector, "w2_scale_rows", R)
         w_scale_rows = zeroed_scales(nc.gpsimd, "w_scale_rows", R)

@@ -59,8 +59,8 @@ def tile_picked_codepage_plain_two_crossgroups_one_plain_kernel(
             engine.memset(held[:].bitcast(I32), 0)
             return held
 
-        def load_scales(held, source, quadrants):
-            for q in quadrants:
+        def load_scales(held, source):
+            for q in range(QUADRANTS):
                 nc.sync.dma_start(
                     out=held[32 * q : 32 * q + 4, :].bitcast(I32),
                     in_=source[0, 4 * q : 4 * q + 4, :].bitcast(I32),
@@ -97,46 +97,45 @@ def tile_picked_codepage_plain_two_crossgroups_one_plain_kernel(
         tables.append(load_table(1))
         reading = load_factor("reading", gb)
         read_list = load_list("read_list", offs3)
-        w2_raw = load_words("w2_raw", w2_words[0].rearrange("p c t -> p (c t)"), R, U32)
-        w_raw = load_words("w_raw", w_words[0], R, U16)
-        load_scales(xo_scale_rows, xo_scales, range(QUADRANTS))
-        load_scales(w2_scale_rows, w2_scales, (0, 1))
-        xo_all = load_words("xo_all", xo_words[0], M, U16)
-        load_scales(w2_scale_rows, w2_scales, (2, 3))
-        note_list = load_list("note_list", offs4)
         tables.append(load_table(2))
+        w_raw = load_words("w_raw", w_words[0], R, U16)
+        w2_raw = load_words("w2_raw", w2_words[0].rearrange("p c t -> p (c t)"), R, U32)
+        xo_all = load_words("xo_all", xo_words[0], M, U16)
+        load_scales(xo_scale_rows, xo_scales)
+        load_scales(w2_scale_rows, w2_scales)
+        note_list = load_list("note_list", offs4)
         tables.append(load_table(3))
-        load_scales(w_scale_rows, w_scales, range(QUADRANTS))
         off_list = load_list("off_list", offs7)
         third_weight = load_factor("third_weight", sd)
         own_list = load_list("own_list", offs5)
         first_weight = load_factor("first_weight", sa)
         shared_list = load_list("shared_list", offs6)
         second_weight = load_factor("second_weight", sb)
+        load_scales(w_scale_rows, w_scales)
         wb_codes = load_words("wb_codes", wb_words[0].rearrange("p c t -> p (c t)"), N, U32)
-        load_scales(wb_scale_rows, wb_scales, range(QUADRANTS))
+        load_scales(wb_scale_rows, wb_scales)
 
-        def fetch_codes(xcd, t):
-            fetch(xcd[:, t % 2, :], tables[t], code_list[:], step, t)
-
-        def put_codes(xcd, t):
-            nc.vector.tensor_copy(out=pages[t][:].indirect(put_list[:]), in_=xcd[:, t % 2, :])
+        def fetch_and_put(t, xcd, pieces):
+            width = J // pieces
+            for piece in range(pieces):
+                slots = slice(width * piece, width * (piece + 1))
+                entries = slice(slots.start // 16, slots.stop // 16)
+                fetch(xcd[:, slots], tables[t], code_list[:, entries], step, t)
+                nc.vector.tensor_copy(out=pages[t][:].indirect(put_list[:, entries]), in_=xcd[:, slots])
 
         def read_page(t):
             for h in range(2):
                 fetch(xc_planes[h][:, t, :], pages[t], read_list[:, 8 * h : 8 * h + 8], reading, t)
 
-        xcd_early = keep.tile([P, 2, J], F32, name="xcd_early")
-        for t in (0, 1):
-            fetch_codes(xcd_early, t)
-            put_codes(xcd_early, t)
-        w2_codes = dealt(nc.scalar.copy, "w2_codes", "w2_codes", w2_raw, U32)
+        for t in range(PACK - 1):
+            fetch_and_put(t, keep.tile([P, J], F32, name="xcd%d" % t), 2 if t == 0 else 1)
         w_codes = dealt(nc.scalar.copy, "w_codes", "w_codes", w_raw, U16)
+        w2_codes = dealt(nc.scalar.copy, "w2_codes", "w2_codes", w2_raw, U32)
         xc_flat = keep.tile([P, PACK * J], BF16, name="xc_flat", tag="w_raw", align_bytes=64)
         xc_planes = [
             xc_flat[:, PACK * HALF * h : PACK * HALF * (h + 1)].rearrange("p (t c) -> p t c", t=PACK) for h in range(2)
         ]
-        for t in (0, 1):
+        for t in range(PACK - 1):
             read_page(t)
 
         w2_plane = dealt(nc.vector.tensor_copy, "w2_plane", "w2_plane", w2_scale_rows, U8)
@@ -144,10 +143,7 @@ def tile_picked_codepage_plain_two_crossgroups_one_plain_kernel(
         nc.vector.tensor_copy(out=note_scales[:], in_=xo_scale_rows[:].indirect(note_list[:]))
         note_codes = keep.tile([P, J], U16, name="note_codes", align_bytes=64)
         nc.vector.tensor_copy(out=note_codes[:], in_=xo_all[:].indirect(note_list[:]))
-        xcd_late = keep.tile([P, 2, J], F32, name="xcd_late", tag="w2_scale_rows", align_bytes=64)
-        for t in (2, 3):
-            fetch_codes(xcd_late, t)
-            put_codes(xcd_late, t)
+        fetch_and_put(PACK - 1, keep.tile([P, J], F32, name="xcd_last", tag="w2_scale_rows", align_bytes=64), 1)
 
         b_rows = []
         for t in range(PACK):
@@ -163,63 +159,82 @@ def tile_picked_codepage_plain_two_crossgroups_one_plain_kernel(
             nc.scalar.copy(out=rows[:], in_=bank[:])
             b_rows.append(rows)
 
-        for t in (2, 3):
-            read_page(t)
+        read_page(PACK - 1)
         w_plane = dealt(nc.vector.tensor_copy, "w_plane", "w2_scale_rows", w_scale_rows, U8)
-        grouped = [keep.tile([P, HALF, PACK], BF16, name="xc_grouped%d" % h, align_bytes=64) for h in range(2)]
+        grouped_flat = keep.tile([P, PACK * J], BF16, name="xc_grouped", tag="w_scale_rows", align_bytes=64)
+        grouped = [grouped_flat[:, PACK * HALF * h : PACK * HALF * (h + 1)] for h in range(2)]
         xc_codes = keep.tile([P, J], U32, name="xc_codes", align_bytes=64)
         xc_scales = keep.tile([P, J], U8, name="xc_scales", align_bytes=64)
         for h in range(2):
             nc.vector.tensor_copy(
-                out=grouped[h][:].rearrange("p (c i) t -> p c t i", i=RUN),
+                out=grouped[h].rearrange("p (c i t) -> p c t i", i=RUN, t=PACK),
                 in_=xc_planes[h].rearrange("p t (c i) -> p c t i", i=RUN),
             )
         for h in range(2):
             nc.vector.quantize_mx(
                 out=xc_codes[:, HALF * h : HALF * (h + 1)].bitcast(FP8X4),
                 scales=xc_scales[:, HALF * h : HALF * (h + 1)],
-                in_=grouped[h][:].rearrange("p c t -> p (c t)"),
+                in_=grouped[h],
             )
 
         taken_off = keep.tile([P, PACK, O], F32, name="taken_off")
         for t in range(PACK):
             fetch(taken_off[:, t, :], b_rows[t], off_list[:], third_weight, t)
 
-        own = keep.tile([P, PACK, O], F32, name="own")
+        own = []
         shared = keep.tile([P, PACK, O], F32, name="shared")
         larger = keep.tile([P, PACK, O], F32, name="larger")
-        for t in range(PACK):
-            cols = slice(P * t, P * (t + 1))
-            bank = psum.tile([P, J], F32, name="a_bank%d" % t, tag="bank%d" % (PACK + t))
-            nc.tensor.matmul_mx(
-                out=bank[:],
-                lhsT=w_codes[:, cols].bitcast(FP4X4), lhsT_scale=w_plane[:, cols],
-                rhs=xc_codes[:].bitcast(FP8X4), rhs_scale=xc_scales[:],
-                start=True, stop=True,
-            )
-            rows = keep.tile([P, J], F32, name="a_rows%d" % t)
-            nc.vector.tensor_copy(out=rows[:], in_=bank[:])
-            fetch(own[:, t, :], rows, own_list[:], first_weight, t)
-            fetch(shared[:, t, :], rows, shared_list[:], second_weight, t)
         hid = keep.tile([P, O, PACK], BF16, name="hid", align_bytes=64)
-        for pair in (slice(0, 2), slice(2, 4)):
-            for t in range(pair.start, pair.stop):
-                nc.vector.tensor_tensor(out=larger[:, t, :], in0=own[:, t, :], in1=shared[:, t, :], op=ALU.max)
-            nc.vector.tensor_tensor(
-                out=hid[:, :, pair].rearrange("p (c i) t -> p c t i", i=RUN),
-                in0=larger[:, pair, :].rearrange("p t (c i) -> p c t i", i=RUN),
-                in1=taken_off[:, pair, :].rearrange("p t (c i) -> p c t i", i=RUN),
-                op=ALU.subtract,
-            )
         hid_codes = keep.tile([P, O], U32, name="hid_codes", align_bytes=64)
         hid_scales = keep.tile([P, O], U8, name="hid_scales", align_bytes=64)
-        nc.vector.quantize_mx(
-            out=hid_codes[:].bitcast(FP8X4), scales=hid_scales[:], in_=hid[:].rearrange("p c t -> p (c t)")
-        )
+
+        def keep_larger(t, places):
+            nc.vector.tensor_tensor(
+                out=larger[:, t, places], in0=own[t][:, places], in1=shared[:, t, places], op=ALU.max
+            )
+
+        def take_off(pair, places):
+            nc.vector.tensor_tensor(
+                out=hid[:, places, pair].rearrange("p (c i) t -> p c t i", i=RUN),
+                in0=larger[:, pair, places].rearrange("p t (c i) -> p c t i", i=RUN),
+                in1=taken_off[:, pair, places].rearrange("p t (c i) -> p c t i", i=RUN),
+                op=ALU.subtract,
+            )
+
+        place_halves = (slice(0, O // 2), slice(O // 2, O))
+        for t in range(PACK):
+            cols = slice(P * t, P * (t + 1))
+            rows = keep.tile([P, J], F32, name="a_rows%d" % t)
+            pieces = ((slice(0, HALF), 0), (slice(HALF, J), PACK)) if t == 0 else ((slice(0, J), PACK + t),)
+            for slots, bank_number in pieces:
+                bank = psum.tile([P, slots.stop - slots.start], F32, name="a_bank", tag="bank%d" % bank_number)
+                nc.tensor.matmul_mx(
+                    out=bank[:],
+                    lhsT=w_codes[:, cols].bitcast(FP4X4), lhsT_scale=w_plane[:, cols],
+                    rhs=xc_codes[:, slots].bitcast(FP8X4), rhs_scale=xc_scales[:, slots],
+                    start=True, stop=True,
+                )
+                nc.vector.tensor_copy(out=rows[:, slots], in_=bank[:])
+            own.append(keep.tile([P, O], F32, name="own%d" % t))
+            fetch(own[t][:], rows, own_list[:], first_weight, t)
+            for places in place_halves if t == PACK - 1 else (slice(0, O),):
+                entries = slice(places.start // 16, places.stop // 16)
+                fetch(shared[:, t, places], rows, shared_list[:, entries], second_weight, t)
+                keep_larger(t, places)
+            if t == 1:
+                take_off(slice(0, 2), slice(0, O))
+
+        for places in place_halves:
+            take_off(slice(2, 4), places)
+        for places in place_halves:
+            nc.vector.quantize_mx(
+                out=hid_codes[:, places].bitcast(FP8X4), scales=hid_scales[:, places],
+                in_=hid[:, places, :].rearrange("p c t -> p (c t)"),
+            )
 
         for h, (copy, queue) in enumerate(((nc.vector.tensor_copy, nc.sync), (nc.scalar.copy, nc.scalar))):
             cols = slice(P * h, P * (h + 1))
-            bank = psum.tile([P, O], F32, name="y_bank%d" % h, tag="bank%d" % h)
+            bank = psum.tile([P, O], F32, name="y_bank%d" % h, tag="bank%d" % (1 + h))
             nc.tensor.matmul_mx(
                 out=bank[:],
                 lhsT=wb_codes[:, cols].bitcast(FP8X4), lhsT_scale=wb_scale_rows[:, cols],

@@ -73,9 +73,10 @@ def tile_picked_codepage_plain_two_crossgroups_one_plain_kernel(
 
         def dealt(copy, name, tag, source, dtype):
             held = keep.tile([P, R], dtype, name=name, tag=tag, align_bytes=64)
+            walk = "p m t" if dtype == U32 else "p t m"
             copy(
-                out=held[:].rearrange("p (t m) -> p m t", t=PACK),
-                in_=source[:].rearrange("p (m t) -> p m t", t=PACK),
+                out=held[:].rearrange("p (t m) -> " + walk, t=PACK),
+                in_=source[:].rearrange("p (m t) -> " + walk, t=PACK),
             )
             return held
 
@@ -193,11 +194,11 @@ def tile_picked_codepage_plain_two_crossgroups_one_plain_kernel(
                 out=larger[:, t, places], in0=own[t][:, places], in1=shared[:, t, places], op=ALU.max
             )
 
-        def take_off(pair, places):
+        def take_off(places):
             nc.vector.tensor_tensor(
-                out=hid[:, places, pair].rearrange("p (c i) t -> p c t i", i=RUN),
-                in0=larger[:, pair, places].rearrange("p t (c i) -> p c t i", i=RUN),
-                in1=taken_off[:, pair, places].rearrange("p t (c i) -> p c t i", i=RUN),
+                out=hid[:, places, :].rearrange("p (c i) t -> p c t i", i=RUN),
+                in0=larger[:, :, places].rearrange("p t (c i) -> p c t i", i=RUN),
+                in1=taken_off[:, :, places].rearrange("p t (c i) -> p c t i", i=RUN),
                 op=ALU.subtract,
             )
 
@@ -221,11 +222,9 @@ def tile_picked_codepage_plain_two_crossgroups_one_plain_kernel(
                 entries = slice(places.start // 16, places.stop // 16)
                 fetch(shared[:, t, places], rows, shared_list[:, entries], second_weight, t)
                 keep_larger(t, places)
-            if t == 1:
-                take_off(slice(0, 2), slice(0, O))
 
         for places in place_halves:
-            take_off(slice(2, 4), places)
+            take_off(places)
         for places in place_halves:
             nc.vector.quantize_mx(
                 out=hid_codes[:, places].bitcast(FP8X4), scales=hid_scales[:, places],

@@ -17,10 +17,19 @@ COPY = mybir.ActivationFunctionType.Copy
 ALU = mybir.AluOpType
 
 P = 128
-PACK = 4
+PLANES = 4
+LAST = PLANES - 1
 QUADRANTS = 4
-HALF = J // 2
+ENTRIES = 16
 RUN = 4
+ALL_SLOTS = slice(0, J)
+SLOT_HALVES = (slice(0, J // 2), slice(J // 2, J))
+ALL_PLACES = slice(0, O)
+PLACE_HALVES = (slice(0, O // 2), slice(O // 2, O))
+
+
+def entries(offsets, part):
+    return offsets[:, part.start // ENTRIES : part.stop // ENTRIES]
 
 
 def tile_picked_codepage_plain_two_crossgroups_one_plain_kernel(
@@ -31,7 +40,6 @@ def tile_picked_codepage_plain_two_crossgroups_one_plain_kernel(
     with ExitStack() as ctx:
         lists = ctx.enter_context(tc.tile_pool(name="lists", bufs=1))
         keep = ctx.enter_context(tc.tile_pool(name="keep", bufs=1))
-        late = ctx.enter_context(tc.tile_pool(name="late", bufs=1))
         psum = ctx.enter_context(tc.psum_pool(name="psum", bufs=1))
 
         def load_list(name, source):
@@ -39,14 +47,14 @@ def tile_picked_codepage_plain_two_crossgroups_one_plain_kernel(
             nc.sync.dma_start(held[:], source)
             return held
 
-        def load_factor(name, source):
-            held = keep.tile([P, PACK], F32, name=name)
-            nc.sync.dma_start(out=held[:], in_=source.rearrange("(p t) one -> p (t one)", t=PACK))
+        def load_factor(name, source, queue):
+            held = keep.tile([P, PLANES], F32, name=name)
+            queue.dma_start(out=held[:], in_=source.rearrange("(p t) one -> p (t one)", t=PLANES))
             return held
 
         def load_table(t):
-            held = late.tile([P, T], F32, name="table%d" % t, offset=4 * T * (PACK - 1 - t))
-            nc.sync.dma_start(out=held[:], in_=ta.rearrange("(p t) c -> p t c", t=PACK)[:, t, :])
+            held = keep.tile([P, T], F32, name="table%d" % t)
+            nc.sync.dma_start(out=held[:], in_=ta.rearrange("(p t) c -> p t c", t=PLANES)[:, t, :])
             return held
 
         def load_words(name, source, columns, dtype):
@@ -54,7 +62,7 @@ def tile_picked_codepage_plain_two_crossgroups_one_plain_kernel(
             nc.sync.dma_start(out=held[:].bitcast(I32), in_=source.bitcast(I32))
             return held
 
-        def zeroed_scales(engine, name, columns):
+        def zeroed_scale_tile(engine, name, columns):
             held = keep.tile([P, columns], U8, name=name, tag=name, align_bytes=64)
             engine.memset(held[:].bitcast(I32), 0)
             return held
@@ -75,171 +83,166 @@ def tile_picked_codepage_plain_two_crossgroups_one_plain_kernel(
             held = keep.tile([P, R], dtype, name=name, tag=tag, align_bytes=64)
             walk = "p m t" if dtype == U32 else "p t m"
             copy(
-                out=held[:].rearrange("p (t m) -> " + walk, t=PACK),
-                in_=source[:].rearrange("p (m t) -> " + walk, t=PACK),
+                out=held[:].rearrange("p (t m) -> " + walk, t=PLANES),
+                in_=source[:].rearrange("p (m t) -> " + walk, t=PLANES),
             )
             return held
 
         idle = keep.tile([P, 16], F32, name="idle")
         nc.gpsimd.memset(idle[:], 0.0)
         nc.scalar.activation(out=idle[:, 8:9], in_=idle[:, 0:1], func=COPY)
-        xo_scale_rows = zeroed_scales(nc.gpsimd, "xo_scale_rows", M)
-        w2_scale_rows = zeroed_scales(nc.vector, "w2_scale_rows", R)
-        w_scale_rows = zeroed_scales(nc.gpsimd, "w_scale_rows", R)
-        wb_scale_rows = zeroed_scales(nc.vector, "wb_scale_rows", N)
-        pages = [keep.tile([P, U], F32, name="page%d" % t) for t in range(PACK)]
+
+        xo_scale_rows = zeroed_scale_tile(nc.gpsimd, "xo_scale_rows", M)
+        w2_scale_rows = zeroed_scale_tile(nc.vector, "w2_scale_rows", R)
+        w_scale_rows = zeroed_scale_tile(nc.gpsimd, "w_scale_rows", R)
+        wb_scale_rows = zeroed_scale_tile(nc.vector, "wb_scale_rows", N)
+        pages = [keep.tile([P, U], F32, name="page%d" % t) for t in range(LAST)]
         for page in pages:
             nc.vector.memset(page[:], 0.0)
 
         tables = [load_table(0)]
         code_list = load_list("code_list", offs)
-        step = load_factor("step", ga)
+        step = load_factor("step", ga, nc.scalar)
         put_list = load_list("put_list", offs2)
         tables.append(load_table(1))
-        reading = load_factor("reading", gb)
+        reading = load_factor("reading", gb, nc.sync)
         read_list = load_list("read_list", offs3)
         tables.append(load_table(2))
+        tables.append(load_table(3))
         w_raw = load_words("w_raw", w_words[0], R, U16)
         w2_raw = load_words("w2_raw", w2_words[0].rearrange("p c t -> p (c t)"), R, U32)
         xo_all = load_words("xo_all", xo_words[0], M, U16)
         load_scales(xo_scale_rows, xo_scales)
         load_scales(w2_scale_rows, w2_scales)
         note_list = load_list("note_list", offs4)
-        tables.append(load_table(3))
         off_list = load_list("off_list", offs7)
-        third_weight = load_factor("third_weight", sd)
+        third_weight = load_factor("third_weight", sd, nc.sync)
         own_list = load_list("own_list", offs5)
-        first_weight = load_factor("first_weight", sa)
+        first_weight = load_factor("first_weight", sa, nc.sync)
         shared_list = load_list("shared_list", offs6)
-        second_weight = load_factor("second_weight", sb)
+        second_weight = load_factor("second_weight", sb, nc.sync)
         load_scales(w_scale_rows, w_scales)
         wb_codes = load_words("wb_codes", wb_words[0].rearrange("p c t -> p (c t)"), N, U32)
         load_scales(wb_scale_rows, wb_scales)
 
-        def fetch_and_put(t, xcd, pieces):
-            width = J // pieces
-            for piece in range(pieces):
-                slots = slice(width * piece, width * (piece + 1))
-                entries = slice(slots.start // 16, slots.stop // 16)
-                fetch(xcd[:, slots], tables[t], code_list[:, entries], step, t)
-                nc.vector.tensor_copy(out=pages[t][:].indirect(put_list[:, entries]), in_=xcd[:, slots])
+        xcd = [keep.tile([P, J], F32, name="xcd%d" % t, tag="xcd%d" % t, align_bytes=64) for t in range(PLANES)]
 
-        def read_page(t):
-            for h in range(2):
-                fetch(xc_planes[h][:, t, :], pages[t], read_list[:, 8 * h : 8 * h + 8], reading, t)
+        def fetch_codes(t, slots):
+            fetch(xcd[t][:, slots], tables[t], entries(code_list, slots), step, t)
 
-        for t in range(PACK - 1):
-            fetch_and_put(t, keep.tile([P, J], F32, name="xcd%d" % t), 2 if t == 0 else 1)
+        def put_codes(t, slots):
+            nc.vector.tensor_copy(out=pages[t][:].indirect(entries(put_list, slots)), in_=xcd[t][:, slots])
+
+        for t in range(LAST):
+            for slots in SLOT_HALVES if t == 0 else (ALL_SLOTS,):
+                fetch_codes(t, slots)
+                put_codes(t, slots)
+        fetch_codes(LAST, ALL_SLOTS)
+
         w_codes = dealt(nc.scalar.copy, "w_codes", "w_codes", w_raw, U16)
         w2_codes = dealt(nc.scalar.copy, "w2_codes", "w2_codes", w2_raw, U32)
-        xc_flat = keep.tile([P, PACK * J], BF16, name="xc_flat", tag="w_raw", align_bytes=64)
+        xc_flat = keep.tile([P, PLANES * J], BF16, name="xc_flat", tag="w_raw", align_bytes=64)
         xc_planes = [
-            xc_flat[:, PACK * HALF * h : PACK * HALF * (h + 1)].rearrange("p (t c) -> p t c", t=PACK) for h in range(2)
+            xc_flat[:, PLANES * slots.start : PLANES * slots.stop].rearrange("p (t c) -> p t c", t=PLANES)
+            for slots in SLOT_HALVES
         ]
-        for t in range(PACK - 1):
+
+        def read_page(t):
+            for half, slots in enumerate(SLOT_HALVES):
+                fetch(xc_planes[half][:, t, :], pages[t], entries(read_list, slots), reading, t)
+
+        for t in range(LAST):
             read_page(t)
 
-        w2_plane = dealt(nc.vector.tensor_copy, "w2_plane", "w2_plane", w2_scale_rows, U8)
+        w2_dealt_scales = dealt(nc.vector.tensor_copy, "w2_dealt_scales", "w2_dealt_scales", w2_scale_rows, U8)
         note_scales = keep.tile([P, J], U8, name="note_scales", align_bytes=64)
         nc.vector.tensor_copy(out=note_scales[:], in_=xo_scale_rows[:].indirect(note_list[:]))
         note_codes = keep.tile([P, J], U16, name="note_codes", align_bytes=64)
         nc.vector.tensor_copy(out=note_codes[:], in_=xo_all[:].indirect(note_list[:]))
-        fetch_and_put(PACK - 1, keep.tile([P, J], F32, name="xcd_last", tag="w2_scale_rows", align_bytes=64), 1)
+        pages.append(keep.tile([P, U], F32, name="last_page", tag="w2_scale_rows", align_bytes=64))
+        nc.gpsimd.memset(pages[LAST][:], 0.0)
+        put_codes(LAST, ALL_SLOTS)
 
         b_rows = []
-        for t in range(PACK):
+        for t in range(PLANES):
             cols = slice(P * t, P * (t + 1))
             bank = psum.tile([P, J], F32, name="b_bank%d" % t, tag="bank%d" % t)
             nc.tensor.matmul_mx(
                 out=bank[:],
-                lhsT=w2_codes[:, cols].bitcast(FP8X4), lhsT_scale=w2_plane[:, cols],
+                lhsT=w2_codes[:, cols].bitcast(FP8X4), lhsT_scale=w2_dealt_scales[:, cols],
                 rhs=note_codes[:].bitcast(FP4X4), rhs_scale=note_scales[:],
                 start=True, stop=True,
             )
-            rows = late.tile([P, J], F32, name="b_rows%d" % t, offset=4 * J * t)
+            rows = keep.tile([P, J], F32, name="b_rows%d" % t)
             nc.scalar.copy(out=rows[:], in_=bank[:])
             b_rows.append(rows)
 
-        read_page(PACK - 1)
-        w_plane = dealt(nc.vector.tensor_copy, "w_plane", "w2_scale_rows", w_scale_rows, U8)
-        grouped_flat = keep.tile([P, PACK * J], BF16, name="xc_grouped", tag="w_scale_rows", align_bytes=64)
-        grouped = [grouped_flat[:, PACK * HALF * h : PACK * HALF * (h + 1)] for h in range(2)]
+        read_page(LAST)
+        w_dealt_scales = dealt(nc.vector.tensor_copy, "w_dealt_scales", "xcd%d" % LAST, w_scale_rows, U8)
+        xc_grouped = keep.tile([P, PLANES * J], BF16, name="xc_grouped", tag="w_scale_rows", align_bytes=64)
+        grouped_halves = [xc_grouped[:, PLANES * slots.start : PLANES * slots.stop] for slots in SLOT_HALVES]
         xc_codes = keep.tile([P, J], U32, name="xc_codes", align_bytes=64)
         xc_scales = keep.tile([P, J], U8, name="xc_scales", align_bytes=64)
-        for h in range(2):
+        for grouped, planes in zip(grouped_halves, xc_planes):
             nc.vector.tensor_copy(
-                out=grouped[h].rearrange("p (c i t) -> p c t i", i=RUN, t=PACK),
-                in_=xc_planes[h].rearrange("p t (c i) -> p c t i", i=RUN),
+                out=grouped.rearrange("p (c i t) -> p c t i", i=RUN, t=PLANES),
+                in_=planes.rearrange("p t (c i) -> p c t i", i=RUN),
             )
-        for h in range(2):
-            nc.vector.quantize_mx(
-                out=xc_codes[:, HALF * h : HALF * (h + 1)].bitcast(FP8X4),
-                scales=xc_scales[:, HALF * h : HALF * (h + 1)],
-                in_=grouped[h],
-            )
+        for grouped, slots in zip(grouped_halves, SLOT_HALVES):
+            nc.vector.quantize_mx(out=xc_codes[:, slots].bitcast(FP8X4), scales=xc_scales[:, slots], in_=grouped)
 
-        taken_off = keep.tile([P, PACK, O], F32, name="taken_off")
-        for t in range(PACK):
+        taken_off = keep.tile([P, PLANES, O], F32, name="taken_off")
+        for t in range(PLANES):
             fetch(taken_off[:, t, :], b_rows[t], off_list[:], third_weight, t)
 
-        own = []
-        shared = keep.tile([P, PACK, O], F32, name="shared")
-        larger = keep.tile([P, PACK, O], F32, name="larger")
-        hid = keep.tile([P, O, PACK], BF16, name="hid", align_bytes=64)
+        shared = keep.tile([P, PLANES, O], F32, name="shared")
+        larger = keep.tile([P, PLANES, O], F32, name="larger")
+        for t in range(PLANES):
+            cols = slice(P * t, P * (t + 1))
+            rows = keep.tile([P, J], F32, name="a_rows%d" % t)
+            pieces = zip(SLOT_HALVES, (0, PLANES)) if t == 0 else ((ALL_SLOTS, PLANES + t),)
+            for slots, bank_number in pieces:
+                bank = psum.tile([P, slots.stop - slots.start], F32, name="a_bank", tag="bank%d" % bank_number)
+                nc.tensor.matmul_mx(
+                    out=bank[:],
+                    lhsT=w_codes[:, cols].bitcast(FP4X4), lhsT_scale=w_dealt_scales[:, cols],
+                    rhs=xc_codes[:, slots].bitcast(FP8X4), rhs_scale=xc_scales[:, slots],
+                    start=True, stop=True,
+                )
+                nc.vector.tensor_copy(out=rows[:, slots], in_=bank[:])
+            own = keep.tile([P, O], F32, name="own%d" % t)
+            fetch(own[:], rows, own_list[:], first_weight, t)
+            for places in PLACE_HALVES if t == LAST else (ALL_PLACES,):
+                fetch(shared[:, t, places], rows, entries(shared_list, places), second_weight, t)
+                nc.vector.tensor_tensor(
+                    out=larger[:, t, places], in0=own[:, places], in1=shared[:, t, places], op=ALU.max
+                )
+
+        hid = keep.tile([P, O, PLANES], BF16, name="hid", align_bytes=64)
         hid_codes = keep.tile([P, O], U32, name="hid_codes", align_bytes=64)
         hid_scales = keep.tile([P, O], U8, name="hid_scales", align_bytes=64)
-
-        def keep_larger(t, places):
-            nc.vector.tensor_tensor(
-                out=larger[:, t, places], in0=own[t][:, places], in1=shared[:, t, places], op=ALU.max
-            )
-
-        def take_off(places):
+        for places in PLACE_HALVES:
             nc.vector.tensor_tensor(
                 out=hid[:, places, :].rearrange("p (c i) t -> p c t i", i=RUN),
                 in0=larger[:, :, places].rearrange("p t (c i) -> p c t i", i=RUN),
                 in1=taken_off[:, :, places].rearrange("p t (c i) -> p c t i", i=RUN),
                 op=ALU.subtract,
             )
-
-        place_halves = (slice(0, O // 2), slice(O // 2, O))
-        for t in range(PACK):
-            cols = slice(P * t, P * (t + 1))
-            rows = keep.tile([P, J], F32, name="a_rows%d" % t)
-            pieces = ((slice(0, HALF), 0), (slice(HALF, J), PACK)) if t == 0 else ((slice(0, J), PACK + t),)
-            for slots, bank_number in pieces:
-                bank = psum.tile([P, slots.stop - slots.start], F32, name="a_bank", tag="bank%d" % bank_number)
-                nc.tensor.matmul_mx(
-                    out=bank[:],
-                    lhsT=w_codes[:, cols].bitcast(FP4X4), lhsT_scale=w_plane[:, cols],
-                    rhs=xc_codes[:, slots].bitcast(FP8X4), rhs_scale=xc_scales[:, slots],
-                    start=True, stop=True,
-                )
-                nc.vector.tensor_copy(out=rows[:, slots], in_=bank[:])
-            own.append(keep.tile([P, O], F32, name="own%d" % t))
-            fetch(own[t][:], rows, own_list[:], first_weight, t)
-            for places in place_halves if t == PACK - 1 else (slice(0, O),):
-                entries = slice(places.start // 16, places.stop // 16)
-                fetch(shared[:, t, places], rows, shared_list[:, entries], second_weight, t)
-                keep_larger(t, places)
-
-        for places in place_halves:
-            take_off(places)
-        for places in place_halves:
+        for places in PLACE_HALVES:
             nc.vector.quantize_mx(
                 out=hid_codes[:, places].bitcast(FP8X4), scales=hid_scales[:, places],
                 in_=hid[:, places, :].rearrange("p c t -> p (c t)"),
             )
 
-        for h, (copy, queue) in enumerate(((nc.vector.tensor_copy, nc.sync), (nc.scalar.copy, nc.scalar))):
-            cols = slice(P * h, P * (h + 1))
-            bank = psum.tile([P, O], F32, name="y_bank%d" % h, tag="bank%d" % (1 + h))
+        for block, (copy, queue) in enumerate(((nc.vector.tensor_copy, nc.sync), (nc.scalar.copy, nc.scalar))):
+            cols = slice(P * block, P * (block + 1))
+            bank = psum.tile([P, O], F32, name="out_bank%d" % block, tag="bank%d" % (1 + block))
             nc.tensor.matmul_mx(
                 out=bank[:],
                 lhsT=wb_codes[:, cols].bitcast(FP8X4), lhsT_scale=wb_scale_rows[:, cols],
                 rhs=hid_codes[:].bitcast(FP8X4), rhs_scale=hid_scales[:],
                 start=True, stop=True,
             )
-            result = keep.tile([P, O], F32, name="result%d" % h)
+            result = keep.tile([P, O], F32, name="result%d" % block)
             copy(out=result[:], in_=bank[:])
             queue.dma_start(out=out[cols, :], in_=result[:])

from contextlib import ExitStack

import concourse.mybir as mybir

K, J, R, T, U, Z, M, O, N = 512, 256, 512, 512, 512, 512, 1024, 128, 256
FLOPS = 2 * (K * R * J + Z * R * J + R * N * O)

F32 = mybir.dt.float32
BF16 = mybir.dt.bfloat16
I32 = mybir.dt.int32
U32 = mybir.dt.uint32
U16 = mybir.dt.uint16
U8 = mybir.dt.uint8
FP8X4 = mybir.dt.float8_e4m3fn_x4
FP4X4 = mybir.dt.float4_e2m1fn_x4
COPY = mybir.ActivationFunctionType.Copy
ALU = mybir.AluOpType

P = 128
PLANES = 4
LAST = PLANES - 1
QUADRANTS = 4
ENTRIES = 16
RUN = 4
ALL_SLOTS = slice(0, J)
SLOT_HALVES = (slice(0, J // 2), slice(J // 2, J))
ALL_PLACES = slice(0, O)
PLACE_HALVES = (slice(0, O // 2), slice(O // 2, O))


def entries(offsets, part):
    return offsets[:, part.start // ENTRIES : part.stop // ENTRIES]


def tile_picked_codepage_plain_two_crossgroups_one_plain_kernel(
    tc, ta, ga, gb, w_words, w_scales, xo_words, xo_scales, w2_words, w2_scales, sa, sb, sd,
    wb_words, wb_scales, offs, offs2, offs3, offs4, offs5, offs6, offs7, out,
):
    nc = tc.nc
    with ExitStack() as ctx:
        lists = ctx.enter_context(tc.tile_pool(name="lists", bufs=1))
        keep = ctx.enter_context(tc.tile_pool(name="keep", bufs=1))
        psum = ctx.enter_context(tc.psum_pool(name="psum", bufs=1))

        def load_list(name, source):
            held = lists.tile(list(source.shape), U16, name=name)
            nc.sync.dma_start(held[:], source)
            return held

        def load_factor(name, source, queue):
            held = keep.tile([P, PLANES], F32, name=name)
            queue.dma_start(out=held[:], in_=source.rearrange("(p t) one -> p (t one)", t=PLANES))
            return held

        def load_table(t):
            held = keep.tile([P, T], F32, name="table%d" % t)
            nc.sync.dma_start(out=held[:], in_=ta.rearrange("(p t) c -> p t c", t=PLANES)[:, t, :])
            return held

        def load_words(name, source, columns, dtype):
            held = keep.tile([P, columns], dtype, name=name, tag=name, align_bytes=64)
            nc.sync.dma_start(out=held[:].bitcast(I32), in_=source.bitcast(I32))
            return held

        def zeroed_scale_tile(engine, name, columns):
            held = keep.tile([P, columns], U8, name=name, tag=name, align_bytes=64)
            engine.memset(held[:].bitcast(I32), 0)
            return held

        def load_scales(held, source):
            for q in range(QUADRANTS):
                nc.sync.dma_start(
                    out=held[32 * q : 32 * q + 4, :].bitcast(I32),
                    in_=source[0, 4 * q : 4 * q + 4, :].bitcast(I32),
                )

        def fetch(target, window, offsets, factor, t):
            nc.scalar.activation(
                out=target, in_=window[:].indirect(offsets), func=COPY, scale=factor[:, t : t + 1]
            )

        def dealt(copy, name, tag, source, dtype):
            held = keep.tile([P, R], dtype, name=name, tag=tag, align_bytes=64)
            walk = "p m t" if dtype == U32 else "p t m"
            copy(
                out=held[:].rearrange("p (t m) -> " + walk, t=PLANES),
                in_=source[:].rearrange("p (m t) -> " + walk, t=PLANES),
            )
            return held

        idle = keep.tile([P, 16], F32, name="idle")
        nc.gpsimd.memset(idle[:], 0.0)
        nc.scalar.activation(out=idle[:, 8:9], in_=idle[:, 0:1], func=COPY)

        xo_scale_rows = zeroed_scale_tile(nc.gpsimd, "xo_scale_rows", M)
        w2_scale_rows = zeroed_scale_tile(nc.vector, "w2_scale_rows", R)
        w_scale_rows = zeroed_scale_tile(nc.gpsimd, "w_scale_rows", R)
        wb_scale_rows = zeroed_scale_tile(nc.vector, "wb_scale_rows", N)
        pages = [keep.tile([P, U], F32, name="page%d" % t) for t in range(LAST)]
        for page in pages:
            nc.vector.memset(page[:], 0.0)

        tables = [load_table(0)]
        code_list = load_list("code_list", offs)
        step = load_factor("step", ga, nc.scalar)
        put_list = load_list("put_list", offs2)
        tables.append(load_table(1))
        reading = load_factor("reading", gb, nc.sync)
        read_list = load_list("read_list", offs3)
        tables.append(load_table(2))
        tables.append(load_table(3))
        w_raw = load_words("w_raw", w_words[0], R, U16)
        w2_raw = load_words("w2_raw", w2_words[0].rearrange("p c t -> p (c t)"), R, U32)
        xo_all = load_words("xo_all", xo_words[0], M, U16)
        load_scales(xo_scale_rows, xo_scales)
        load_scales(w2_scale_rows, w2_scales)
        note_list = load_list("note_list", offs4)
        off_list = load_list("off_list", offs7)
        third_weight = load_factor("third_weight", sd, nc.sync)
        own_list = load_list("own_list", offs5)
        first_weight = load_factor("first_weight", sa, nc.sync)
        shared_list = load_list("shared_list", offs6)
        second_weight = load_factor("second_weight", sb, nc.sync)
        load_scales(w_scale_rows, w_scales)
        wb_codes = load_words("wb_codes", wb_words[0].rearrange("p c t -> p (c t)"), N, U32)
        load_scales(wb_scale_rows, wb_scales)

        xcd = [keep.tile([P, J], F32, name="xcd%d" % t, tag="xcd%d" % t, align_bytes=64) for t in range(PLANES)]

        def fetch_codes(t, slots):
            fetch(xcd[t][:, slots], tables[t], entries(code_list, slots), step, t)

        def put_codes(t, slots):
            nc.vector.tensor_copy(out=pages[t][:].indirect(entries(put_list, slots)), in_=xcd[t][:, slots])

        for t in range(LAST):
            for slots in SLOT_HALVES if t == 0 else (ALL_SLOTS,):
                fetch_codes(t, slots)
                put_codes(t, slots)
        fetch_codes(LAST, ALL_SLOTS)

        w_codes = dealt(nc.scalar.copy, "w_codes", "w_codes", w_raw, U16)
        w2_codes = dealt(nc.scalar.copy, "w2_codes", "w2_codes", w2_raw, U32)
        xc_flat = keep.tile([P, PLANES * J], BF16, name="xc_flat", tag="w_raw", align_bytes=64)
        xc_planes = [
            xc_flat[:, PLANES * slots.start : PLANES * slots.stop].rearrange("p (t c) -> p t c", t=PLANES)
            for slots in SLOT_HALVES
        ]

        def read_page(t):
            for half, slots in enumerate(SLOT_HALVES):
                fetch(xc_planes[half][:, t, :], pages[t], entries(read_list, slots), reading, t)

        for t in range(LAST):
            read_page(t)

        w2_dealt_scales = dealt(nc.vector.tensor_copy, "w2_dealt_scales", "w2_dealt_scales", w2_scale_rows, U8)
        note_scales = keep.tile([P, J], U8, name="note_scales", align_bytes=64)
        nc.vector.tensor_copy(out=note_scales[:], in_=xo_scale_rows[:].indirect(note_list[:]))
        note_codes = keep.tile([P, J], U16, name="note_codes", align_bytes=64)
        nc.vector.tensor_copy(out=note_codes[:], in_=xo_all[:].indirect(note_list[:]))
        pages.append(keep.tile([P, U], F32, name="last_page", tag="w2_scale_rows", align_bytes=64))
        nc.gpsimd.memset(pages[LAST][:], 0.0)
        put_codes(LAST, ALL_SLOTS)

        b_rows = []
        for t in range(PLANES):
            cols = slice(P * t, P * (t + 1))
            bank = psum.tile([P, J], F32, name="b_bank%d" % t, tag="bank%d" % t)
            nc.tensor.matmul_mx(
                out=bank[:],
                lhsT=w2_codes[:, cols].bitcast(FP8X4), lhsT_scale=w2_dealt_scales[:, cols],
                rhs=note_codes[:].bitcast(FP4X4), rhs_scale=note_scales[:],
                start=True, stop=True,
            )
            rows = keep.tile([P, J], F32, name="b_rows%d" % t)
            nc.scalar.copy(out=rows[:], in_=bank[:])
            b_rows.append(rows)

        read_page(LAST)
        w_dealt_scales = dealt(nc.vector.tensor_copy, "w_dealt_scales", "xcd%d" % LAST, w_scale_rows, U8)
        xc_grouped = keep.tile([P, PLANES * J], BF16, name="xc_grouped", tag="w_scale_rows", align_bytes=64)
        grouped_halves = [xc_grouped[:, PLANES * slots.start : PLANES * slots.stop] for slots in SLOT_HALVES]
        xc_codes = keep.tile([P, J], U32, name="xc_codes", align_bytes=64)
        xc_scales = keep.tile([P, J], U8, name="xc_scales", align_bytes=64)
        for grouped, planes in zip(grouped_halves, xc_planes):
            nc.vector.tensor_copy(
                out=grouped.rearrange("p (c i t) -> p c t i", i=RUN, t=PLANES),
                in_=planes.rearrange("p t (c i) -> p c t i", i=RUN),
            )
        for grouped, slots in zip(grouped_halves, SLOT_HALVES):
            nc.vector.quantize_mx(out=xc_codes[:, slots].bitcast(FP8X4), scales=xc_scales[:, slots], in_=grouped)

        taken_off = keep.tile([P, PLANES, O], F32, name="taken_off")
        for t in range(PLANES):
            fetch(taken_off[:, t, :], b_rows[t], off_list[:], third_weight, t)

        shared = keep.tile([P, PLANES, O], F32, name="shared")
        larger = keep.tile([P, PLANES, O], F32, name="larger")
        for t in range(PLANES):
            cols = slice(P * t, P * (t + 1))
            rows = keep.tile([P, J], F32, name="a_rows%d" % t)
            pieces = zip(SLOT_HALVES, (0, PLANES)) if t == 0 else ((ALL_SLOTS, PLANES + t),)
            for slots, bank_number in pieces:
                bank = psum.tile([P, slots.stop - slots.start], F32, name="a_bank", tag="bank%d" % bank_number)
                nc.tensor.matmul_mx(
                    out=bank[:],
                    lhsT=w_codes[:, cols].bitcast(FP4X4), lhsT_scale=w_dealt_scales[:, cols],
                    rhs=xc_codes[:, slots].bitcast(FP8X4), rhs_scale=xc_scales[:, slots],
                    start=True, stop=True,
                )
                nc.vector.tensor_copy(out=rows[:, slots], in_=bank[:])
            own = keep.tile([P, O], F32, name="own%d" % t)
            fetch(own[:], rows, own_list[:], first_weight, t)
            for places in PLACE_HALVES if t == LAST else (ALL_PLACES,):
                fetch(shared[:, t, places], rows, entries(shared_list, places), second_weight, t)
                nc.vector.tensor_tensor(
                    out=larger[:, t, places], in0=own[:, places], in1=shared[:, t, places], op=ALU.max
                )

        hid = keep.tile([P, O, PLANES], BF16, name="hid", align_bytes=64)
        hid_codes = keep.tile([P, O], U32, name="hid_codes", align_bytes=64)
        hid_scales = keep.tile([P, O], U8, name="hid_scales", align_bytes=64)
        for places in PLACE_HALVES:
            nc.vector.tensor_tensor(
                out=hid[:, places, :].rearrange("p (c i) t -> p c t i", i=RUN),
                in0=larger[:, :, places].rearrange("p t (c i) -> p c t i", i=RUN),
                in1=taken_off[:, :, places].rearrange("p t (c i) -> p c t i", i=RUN),
                op=ALU.subtract,
            )
        for places in PLACE_HALVES:
            nc.vector.quantize_mx(
                out=hid_codes[:, places].bitcast(FP8X4), scales=hid_scales[:, places],
                in_=hid[:, places, :].rearrange("p c t -> p (c t)"),
            )

        for block, (copy, queue) in enumerate(((nc.vector.tensor_copy, nc.sync), (nc.scalar.copy, nc.scalar))):
            cols = slice(P * block, P * (block + 1))
            bank = psum.tile([P, O], F32, name="out_bank%d" % block, tag="bank%d" % (1 + block))
            nc.tensor.matmul_mx(
                out=bank[:],
                lhsT=wb_codes[:, cols].bitcast(FP8X4), lhsT_scale=wb_scale_rows[:, cols],
                rhs=hid_codes[:].bitcast(FP8X4), rhs_scale=hid_scales[:],
                start=True, stop=True,
            )
            result = keep.tile([P, O], F32, name="result%d" % block)
            copy(out=result[:], in_=bank[:])
            queue.dma_start(out=out[cols, :], in_=result[:])
